import numpy as np
import ml_dtypes


def mxq(x, axis, fmt="e4m3"):
    dtype, down = {"e4m3": (ml_dtypes.float8_e4m3fn, 7), "e5m2": (ml_dtypes.float8_e5m2, 14)}[fmt]
    v = np.moveaxis(np.asarray(x, np.float32).astype(ml_dtypes.bfloat16).astype(np.float64), axis, -1)
    blocks = v.reshape(v.shape[:-1] + (-1, 32))
    amax = np.abs(blocks).max(-1, keepdims=True)
    byte = np.maximum(np.where(amax > 0, np.frexp(amax)[1] - 1 + 127, 0) - down, 1)
    scale = np.exp2(byte - 127.0)
    codes = (blocks / scale).astype(np.float32).astype(dtype).astype(np.float64)
    return np.moveaxis((codes * scale).reshape(v.shape), -1, axis)


WIDE = False


def mx_kscale(k):
    if not WIDE:
        return np.ones(k)
    levels = np.array([10, -10, 5, -5, 0])
    if k % 512:
        return np.exp2(np.random.permutation(np.resize(levels, k // 32))).repeat(32)
    a = np.empty((k // 512, 16))
    for p in range(k // 512):
        a[p, :8] = np.random.permutation(np.resize(levels, 8))
        for g in range(8):
            far = levels[np.abs(levels - a[p, g]) >= 10]
            a[p, g + 8] = far[np.random.randint(len(far))]
    return np.exp2(a.ravel()).repeat(32)


def f64(x):
    return np.asarray(x).astype(np.float64)


def striped(idx):
    return np.tile(idx.reshape(-1, 16).T, (8, 1)).astype(np.uint16)


def unstriped(offs):
    return offs[:16].T.reshape(-1).astype(np.int64)


def striped8(idx):
    return np.concatenate([x.reshape(-1, 16).T for x in idx]).astype(np.uint16)


def runs(offs, k):
    lists = np.stack([offs[16 * r : 16 * r + 16].T.reshape(-1) for r in range(8)]).astype(np.int64)
    return lists[np.arange(k) % 512 // 64]


def pack_weight(w):
    k, n = w.shape
    w = f64(np.asarray(w, np.float32).astype(ml_dtypes.bfloat16)).reshape(k // 32, 32, n)
    amax = np.abs(w).max(1)
    byte = np.clip(np.where(amax > 0, np.frexp(amax)[1] - 1 + 127 - 7, 1), 1, 254)
    scaled = (w * np.exp2(127.0 - byte)[:, None, :]).reshape(k, n).astype(np.float32)
    words = np.ascontiguousarray(scaled.reshape(k // 512, 128, 4, n).transpose(0, 1, 3, 2)).astype(ml_dtypes.float8_e4m3fn).view(np.uint8)
    return words, np.ascontiguousarray(byte.astype(np.uint8).reshape(k // 512, 16, n))


def unpack_weight(words, scales):
    g, p, n, _ = words.shape
    vals = np.ascontiguousarray(words).view(ml_dtypes.float8_e4m3fn).astype(np.float64) * np.repeat(np.exp2(scales.astype(np.float64) - 127.0), 8, axis=1)[..., None]
    return vals.transpose(0, 1, 3, 2).reshape(g * 512, n)


def sigmoid(v):
    return 1.0 / (1.0 + np.exp(-np.maximum(v, -700.0)))


K, T, S, N, H, W = 512, 2048, 512, 512, 512, 256


def setup_inputs():
    n = np.random.standard_normal
    s = mx_kscale(K)[:, None]
    u = mx_kscale(H)
    packed_xT = pack_weight(n((K, T)) * s)
    perm = np.random.permutation(S)
    return {
        "x_words": packed_xT[0],
        "x_scales": packed_xT[1],
        "w1": (n((K, H)) / np.sqrt(K) / s).astype(np.float32),
        "gn": (np.random.uniform(0.5, 1.5, (H, 1)) * u[:, None]).astype(np.float32),
        "w2": (n((H, N)) / np.sqrt(2 * H) / u[:, None]).astype(np.float32),
        "w3": (n((K, N)) / np.sqrt(2 * K) / s).astype(np.float32),
        "tau": np.random.uniform(0.3, 0.9, (N, 1)).astype(np.float32),
        "tau2": np.random.uniform(0.3, 0.9, (N, 1)).astype(np.float32),
        "offs": striped8(np.random.randint(0, T, (8, S))),
        "n1": striped(perm[:W]),
        "n2": striped(perm[W:]),
        "two": striped(np.random.permutation(T)[:S]),
        "n3": striped8(np.stack([np.random.permutation(S) for _ in range(8)])),
        "n4": striped8(np.stack([np.random.permutation(S) for _ in range(8)])),
    }


def reference(x_words, x_scales, w1, gn, w2, w3, tau, tau2, offs, n1, n2, two, n3, n4):
    xq = unpack_weight(x_words, x_scales)[np.arange(K)[:, None], runs(offs, K)]
    y = mxq(f64(w1), 0, "e4m3").T @ xq
    pa = y[:, unstriped(n1)]
    pb = y[:, unstriped(n2)]
    ra = pa * sigmoid(pb)
    ds = y.copy()
    ds[:, unstriped(n2)] = ra
    z = f64(gn) * ds
    x_two = unpack_weight(x_words, x_scales)[:, unstriped(two)]
    h = mxq(f64(w2), 0, "e4m3").T @ mxq(z, 0, "e4m3") + mxq(f64(w3), 0, "e4m3").T @ x_two
    top = h.max(axis=1, keepdims=True)
    ea = np.exp(f64(tau) * (h[np.arange(N)[:, None], runs(n3, N)] - top))
    low = h.min(axis=1, keepdims=True)
    ea2 = np.exp(f64(tau2) * (low - (h[np.arange(N)[:, None], runs(n4, N)])))
    return 1.5 * (h * (ea + ea2))

@@ -1,0 +1,259 @@
+from contextlib import ExitStack
+
+import concourse.mybir as mybir
+
+K, T, S, N, H, W = 512, 2048, 512, 512, 512, 256
+FLOPS = 2 * S * (K * H + H * N + K * N)
+
+F32 = mybir.dt.float32
+BF16 = mybir.dt.bfloat16
+I32 = mybir.dt.int32
+U32 = mybir.dt.uint32
+U16 = mybir.dt.uint16
+U8 = mybir.dt.uint8
+FP8X4 = mybir.dt.float8_e4m3fn_x4
+ALU = mybir.AluOpType
+ACT = mybir.ActivationFunctionType
+
+P = 128
+PACK = 4
+HALF = 256
+
+
+def tile_picked_hmixfoldedf_none_p_kernel(
+    tc, x_words, x_scales, w1, gn, w2, w3, tau, tau2, offs, n1, n2, two, n3, n4, out
+):
+    nc = tc.nc
+    with ExitStack() as ctx:
+        keep = ctx.enter_context(tc.tile_pool(name="keep", bufs=1))
+        psum = ctx.enter_context(tc.psum_pool(name="psum", bufs=1))
+
+        def load_list(name, src):
+            dst = keep.tile(list(src.shape), U16, name=name)
+            nc.sync.dma_start(dst[:], src)
+            return dst
+
+        def load_weight(name, src):
+            dst = keep.tile([P, PACK, src.shape[1]], F32, name=name)
+            nc.sync.dma_start(dst[:], src.rearrange("(p j) c -> p j c", j=PACK))
+            return dst
+
+        def load_rows(name, src):
+            dst = keep.tile([P, PACK], F32, name=name)
+            nc.gpsimd.dma_start(dst[:], src.rearrange("(p t) o -> p (t o)", t=PACK))
+            return dst
+
+        x_bytes = keep.tile([P, T], U8, name="x_bytes")
+        nc.vector.memset(x_bytes[:].bitcast(I32), 0)
+        nc.scalar.dma_start(x_bytes[0:P:8, :].bitcast(I32), x_scales[0].bitcast(I32))
+
+        offs_l = load_list("offs_l", offs)
+        two_l = load_list("two_l", two)
+        x_codes = keep.tile([P, T], U32, name="x_codes")
+        nc.sync.dma_start(
+            x_codes[:].bitcast(I32), x_words[0].rearrange("p n r -> p (n r)").bitcast(I32)
+        )
+        n2_l = load_list("n2_l", n2)
+        n1_l = load_list("n1_l", n1)
+        n3_l = load_list("n3_l", n3)
+        w1_raw = [load_weight(f"w1_raw{c}", w1[:, c * HALF : (c + 1) * HALF]) for c in range(2)]
+        n4_l = load_list("n4_l", n4)
+        w2_raw = load_weight("w2_raw", w2)
+        w3_raw = load_weight("w3_raw", w3)
+        gain = load_rows("gain", gn)
+        rate = load_rows("rate", tau)
+        rate2 = load_rows("rate2", tau2)
+
+        h_rows = [keep.tile([P, 2 * S], F32, name=f"h_rows{t}") for t in range(PACK)]
+        for t in range(PACK):
+            nc.vector.memset(h_rows[t][:, S:], 0.0)
+
+        neg_rate = keep.tile([P, PACK], F32, name="neg_rate")
+        neg_rate2 = keep.tile([P, PACK], F32, name="neg_rate2")
+        nc.gpsimd.tensor_scalar(neg_rate[:], rate[:], -1.0, 0.0, ALU.mult, ALU.add)
+        nc.gpsimd.tensor_scalar(neg_rate2[:], rate2[:], -1.0, 0.0, ALU.mult, ALU.add)
+
+        picked_bytes = keep.tile([P, 2 * S], U8, name="picked_bytes")
+        nc.vector.tensor_copy(picked_bytes[:, :S], x_bytes[:].indirect(offs_l[:]))
+        nc.vector.tensor_copy(picked_bytes[:, S:], x_bytes[:].indirect(two_l[:]))
+        x_planes = keep.tile([P, 2 * S], U8, name="x_planes", align_bytes=64)
+        nc.vector.tensor_copy(x_planes[:].bitcast(I32), picked_bytes[:].bitcast(I32))
+        for r in range(1, 4):
+            nc.scalar.dma_start(
+                x_planes[r:P:32, :].bitcast(I32), picked_bytes[8 * r : P : 32, :].bitcast(I32)
+            )
+
+        xq_codes = keep.tile([P, S], U32, name="xq_codes", align_bytes=64)
+        nc.vector.tensor_copy(xq_codes[:], x_codes[:].indirect(offs_l[:]))
+
+        two_codes = keep.tile([P, S], U32, name="two_codes", align_bytes=64)
+        nc.vector.tensor_copy(two_codes[:], x_codes[:].indirect(two_l[:]))
+
+        def deal(copy, grouped, raw, t0, t1):
+            copy(
+                grouped.rearrange("p t m j -> p m j t"),
+                raw[:].rearrange("p j (m t) -> p m j t", t=PACK)[:, :, :, t0:t1],
+            )
+
+        def quantize(codes, scales, grouped):
+            nc.vector.quantize_mx(out=codes.bitcast(FP8X4), scales=scales, in_=grouped)
+
+        w1_grouped = [
+            keep.tile([P, PACK, 64, PACK], BF16, name=f"w1_grouped{c}", align_bytes=64) for c in range(2)
+        ]
+        deal(nc.scalar.copy, w1_grouped[0][:], w1_raw[0], 0, 4)
+        deal(nc.scalar.copy, w1_grouped[1][:, 0:2], w1_raw[1], 0, 2)
+        deal(nc.scalar.copy, w1_grouped[1][:, 2:4], w1_raw[1], 2, 4)
+        w1_codes = keep.tile([P, H], U32, name="w1_codes", align_bytes=64)
+        w1_scales = keep.tile([P, H], U8, name="w1_scales", align_bytes=64)
+        y_banks = []
+        for t in range(PACK):
+            for c in range(2):
+                cols = slice(t * P + c * 64, t * P + (c + 1) * 64)
+                quantize(
+                    w1_codes[:, cols], w1_scales[:, cols], w1_grouped[c][:, t].rearrange("p m j -> p (m j)")
+                )
+            cols = slice(t * P, (t + 1) * P)
+            bank = psum.tile([P, S], F32, name=f"y_bank{t}")
+            nc.tensor.matmul_mx(
+                out=bank[:],
+                lhsT=w1_codes[:, cols].bitcast(FP8X4),
+                lhsT_scale=w1_scales[:, cols],
+                rhs=xq_codes[:].bitcast(FP8X4),
+                rhs_scale=x_planes[:, :S],
+                start=True,
+                stop=True,
+            )
+            y_banks.append(bank)
+
+        w2_grouped = keep.tile([P, PACK, P, PACK], BF16, name="w2_grouped", align_bytes=64)
+        w2_codes = keep.tile([P, N], U32, name="w2_codes", align_bytes=64)
+        w2_scales = keep.tile([P, N], U8, name="w2_scales", align_bytes=64)
+        w3_codes = keep.tile([P, N], U32, name="w3_codes", align_bytes=64)
+        w3_scales = keep.tile([P, N], U8, name="w3_scales", align_bytes=64)
+
+        z_pairs = keep.tile([P, 2, S, 2], BF16, name="z_pairs")
+        ds_rows = []
+
+        def apply_gain(t):
+            nc.vector.tensor_scalar(
+                z_pairs[:, t // 2, :, t % 2], ds_rows[t][:], gain[:, t : t + 1], None, ALU.mult
+            )
+
+        for t in range(PACK):
+            ds = keep.tile([P, S], F32, name=f"ds{t}")
+            ds_rows.append(ds)
+            if t == 0:
+                nc.vector.tensor_copy(ds[:], y_banks[t][:])
+                deal(nc.vector.tensor_copy, w2_grouped[:], w2_raw, 0, 4)
+                quantize(w2_codes[:], w2_scales[:], w2_grouped[:].rearrange("p t m j -> p (t m j)"))
+            else:
+                nc.scalar.copy(ds[:], y_banks[t][:])
+            gate = keep.tile([P, W], F32, name=f"gate{t}")
+            pa = keep.tile([P, W], F32, name=f"pa{t}")
+            nc.scalar.activation(gate[:], ds[:].indirect(n2_l[:]), ACT.Sigmoid)
+            nc.scalar.activation(pa[:], ds[:].indirect(n1_l[:]), ACT.Copy)
+            if t == 2:
+                ra = keep.tile([P, W], F32, name="ra")
+                nc.vector.tensor_tensor(ra[:], pa[:], gate[:], ALU.mult)
+            else:
+                nc.vector.tensor_tensor(ds[:].indirect(n2_l[:]), pa[:], gate[:], ALU.mult)
+            if t == 3:
+                nc.scalar.activation(ds_rows[2][:].indirect(n2_l[:]), ra[:], ACT.Copy)
+                apply_gain(2)
+            if t != 2:
+                apply_gain(t)
+
+        w3_low = keep.tile([P, 2, P, PACK], BF16, name="w3_low", align_bytes=64)
+        deal(nc.scalar.copy, w3_low[:], w3_raw, 0, 2)
+        quantize(w3_codes[:, :HALF], w3_scales[:, :HALF], w3_low[:].rearrange("p t m j -> p (t m j)"))
+
+        z_grouped = keep.tile([P, S * PACK], BF16, name="z_grouped", tag="late", align_bytes=64)
+        nc.vector.tensor_copy(
+            z_grouped[:].bitcast(I32).rearrange("p (c u) -> p c u", u=2),
+            z_pairs[:].rearrange("p u c e -> p u (c e)").bitcast(I32).rearrange("p u c -> p c u"),
+        )
+        z_codes = keep.tile([P, S], U32, name="z_codes", align_bytes=64)
+        z_scales = keep.tile([P, S], U8, name="z_scales", align_bytes=64)
+        quantize(z_codes[:], z_scales[:], z_grouped[:])
+
+        h_banks = [psum.tile([P, S], F32, name=f"h_bank{t}") for t in range(PACK)]
+
+        def plain_pass(t):
+            cols = slice(t * P, (t + 1) * P)
+            nc.tensor.matmul_mx(
+                out=h_banks[t][:],
+                lhsT=w3_codes[:, cols].bitcast(FP8X4),
+                lhsT_scale=w3_scales[:, cols],
+                rhs=two_codes[:].bitcast(FP8X4),
+                rhs_scale=x_planes[:, S:],
+                start=True,
+                stop=False,
+            )
+
+        def hidden_pass(t):
+            cols = slice(t * P, (t + 1) * P)
+            nc.tensor.matmul_mx(
+                out=h_banks[t][:],
+                lhsT=w2_codes[:, cols].bitcast(FP8X4),
+                lhsT_scale=w2_scales[:, cols],
+                rhs=z_codes[:].bitcast(FP8X4),
+                rhs_scale=z_scales[:],
+                start=False,
+                stop=True,
+            )
+
+        biases = []
+
+        def row_stats(t):
+            stats = keep.tile([P, 4], F32, name=f"stats{t}")
+            top, low, bias, bias2 = (stats[:, i : i + 1] for i in range(4))
+            nc.vector.tensor_scalar(
+                h_rows[t][:, :S], h_banks[t][:], 1.0, None, ALU.mult, ALU.max, accum_out=top
+            )
+            nc.vector.tensor_scalar(bias, top, neg_rate[:, t : t + 1], None, ALU.mult)
+            nc.vector.tensor_reduce(low, h_banks[t][:], mybir.AxisListType.X, ALU.min)
+            nc.vector.tensor_scalar(bias2, low, rate2[:, t : t + 1], None, ALU.mult)
+            biases.append((bias, bias2))
+
+        plain_pass(0)
+        plain_pass(1)
+        hidden_pass(0)
+        hidden_pass(1)
+        w3_high = keep.tile([P, 2, P, PACK], BF16, name="w3_high", tag="late", align_bytes=64)
+        deal(nc.vector.tensor_copy, w3_high[:], w3_raw, 2, 4)
+        row_stats(0)
+        quantize(w3_codes[:, HALF:], w3_scales[:, HALF:], w3_high[:].rearrange("p t m j -> p (t m j)"))
+        for t in (2, 3):
+            plain_pass(t)
+            hidden_pass(t)
+        for t in (1, 2, 3):
+            row_stats(t)
+
+        out_rows = out.rearrange("(p t) n -> t p n", t=PACK)
+        for t in range(PACK):
+            bias, bias2 = biases[t]
+            ea = keep.tile([P, S], F32, name=f"ea{t}")
+            nc.scalar.activation(
+                ea[:], h_rows[t][:].indirect(n3_l[:]), ACT.Exp, bias=bias, scale=rate[:, t : t + 1]
+            )
+            pieces = 2 if t == PACK - 1 else 1
+            width = S // pieces
+            for i in range(pieces):
+                cols = slice(i * width, (i + 1) * width)
+                ea2 = keep.tile([P, width], F32, name=f"ea2_{t}_{i}")
+                nc.scalar.activation(
+                    ea2[:],
+                    h_rows[t][:].indirect(n4_l[:, i * width // 16 : (i + 1) * width // 16]),
+                    ACT.Exp,
+                    bias=bias2,
+                    scale=neg_rate2[:, t : t + 1],
+                )
+                both = keep.tile([P, width], F32, name=f"both_{t}_{i}")
+                adder = nc.vector if t == PACK - 1 else nc.gpsimd
+                adder.tensor_tensor(both[:], ea[:, cols], ea2[:], ALU.add)
+                result = keep.tile([P, width], F32, name=f"result_{t}_{i}")
+                nc.vector.scalar_tensor_tensor(
+                    result[:], h_banks[t][:, cols], 1.5, both[:], ALU.mult, ALU.mult
+                )
+                nc.sync.dma_start(out_rows[t][:, cols], result[:])

@@ -33,8 +33,8 @@ def tile_picked_hmixfoldedf_none_p_kernel(
             nc.sync.dma_start(dst[:], src)
             return dst
 
-        def load_weight(name, src):
-            dst = keep.tile([P, PACK, src.shape[1]], F32, name=name)
+        def load_weight(name, src, tag):
+            dst = keep.tile([P, PACK, src.shape[1]], F32, name=name, tag=tag)
             nc.sync.dma_start(dst[:], src.rearrange("(p j) c -> p j c", j=PACK))
             return dst
 
@@ -43,7 +43,7 @@ def tile_picked_hmixfoldedf_none_p_kernel(
             nc.gpsimd.dma_start(dst[:], src.rearrange("(p t) o -> p (t o)", t=PACK))
             return dst
 
-        x_bytes = keep.tile([P, T], U8, name="x_bytes")
+        x_bytes = keep.tile([P, T], U8, name="x_bytes", tag="bytes_then_w2")
         nc.vector.memset(x_bytes[:].bitcast(I32), 0)
         nc.scalar.dma_start(x_bytes[0:P:8, :].bitcast(I32), x_scales[0].bitcast(I32))
 
@@ -55,11 +55,9 @@ def tile_picked_hmixfoldedf_none_p_kernel(
         )
         n2_l = load_list("n2_l", n2)
         n1_l = load_list("n1_l", n1)
-        n3_l = load_list("n3_l", n3)
-        w1_raw = [load_weight(f"w1_raw{c}", w1[:, c * HALF : (c + 1) * HALF]) for c in range(2)]
-        n4_l = load_list("n4_l", n4)
-        w2_raw = load_weight("w2_raw", w2)
-        w3_raw = load_weight("w3_raw", w3)
+        w1_raw = [
+            load_weight(f"w1_raw{c}", w1[:, c * HALF : (c + 1) * HALF], f"w1_raw{c}") for c in range(2)
+        ]
         gain = load_rows("gain", gn)
         rate = load_rows("rate", tau)
         rate2 = load_rows("rate2", tau2)
@@ -68,26 +66,39 @@ def tile_picked_hmixfoldedf_none_p_kernel(
         for t in range(PACK):
             nc.vector.memset(h_rows[t][:, S:], 0.0)
 
+        warm = keep.tile([P, 1], F32, name="warm")
+        nc.scalar.activation(warm[:], h_rows[0][:, S : S + 1], ACT.Sigmoid)
+
         neg_rate = keep.tile([P, PACK], F32, name="neg_rate")
         neg_rate2 = keep.tile([P, PACK], F32, name="neg_rate2")
         nc.gpsimd.tensor_scalar(neg_rate[:], rate[:], -1.0, 0.0, ALU.mult, ALU.add)
         nc.gpsimd.tensor_scalar(neg_rate2[:], rate2[:], -1.0, 0.0, ALU.mult, ALU.add)
 
-        picked_bytes = keep.tile([P, 2 * S], U8, name="picked_bytes")
-        nc.vector.tensor_copy(picked_bytes[:, :S], x_bytes[:].indirect(offs_l[:]))
-        nc.vector.tensor_copy(picked_bytes[:, S:], x_bytes[:].indirect(two_l[:]))
-        x_planes = keep.tile([P, 2 * S], U8, name="x_planes", align_bytes=64)
-        nc.vector.tensor_copy(x_planes[:].bitcast(I32), picked_bytes[:].bitcast(I32))
-        for r in range(1, 4):
-            nc.scalar.dma_start(
-                x_planes[r:P:32, :].bitcast(I32), picked_bytes[8 * r : P : 32, :].bitcast(I32)
-            )
+        def pick_bytes(name, offsets, tag):
+            picked = keep.tile([P, S], U8, name=name, tag=tag)
+            nc.vector.tensor_copy(picked[:], x_bytes[:].indirect(offsets[:]))
+            return picked
 
-        xq_codes = keep.tile([P, S], U32, name="xq_codes", align_bytes=64)
-        nc.vector.tensor_copy(xq_codes[:], x_codes[:].indirect(offs_l[:]))
+        def place_bytes(name, picked, queue):
+            plane = keep.tile([P, S], U8, name=name, align_bytes=64)
+            nc.vector.memset(plane[:].bitcast(I32), 0)
+            for r in range(4):
+                queue.dma_start(plane[r:P:32, :].bitcast(I32), picked[8 * r : P : 32, :].bitcast(I32))
+            return plane
 
-        two_codes = keep.tile([P, S], U32, name="two_codes", align_bytes=64)
-        nc.vector.tensor_copy(two_codes[:], x_codes[:].indirect(two_l[:]))
+        def pick_words(name, offsets):
+            codes = keep.tile([P, S], U32, name=name, align_bytes=64)
+            nc.vector.tensor_copy(codes[:], x_codes[:].indirect(offsets[:]))
+            return codes
+
+        xq_scales = place_bytes("xq_scales", pick_bytes("xq_picked", offs_l, "bytes_then_w3"), nc.scalar)
+        two_picked = pick_bytes("two_picked", two_l, "two_picked")
+        xq_codes = pick_words("xq_codes", offs_l)
+        w2_raw = load_weight("w2_raw", w2, "bytes_then_w2")
+        w3_raw = load_weight("w3_raw", w3, "bytes_then_w3")
+        two_scales = place_bytes("two_scales", two_picked, nc.sync)
+        n3_l = load_list("n3_l", n3)
+        n4_l = load_list("n4_l", n4)
 
         def deal(copy, grouped, raw, t0, t1):
             copy(
@@ -120,7 +131,7 @@ def tile_picked_hmixfoldedf_none_p_kernel(
                 lhsT=w1_codes[:, cols].bitcast(FP8X4),
                 lhsT_scale=w1_scales[:, cols],
                 rhs=xq_codes[:].bitcast(FP8X4),
-                rhs_scale=x_planes[:, :S],
+                rhs_scale=xq_scales[:],
                 start=True,
                 stop=True,
             )
@@ -134,6 +145,8 @@ def tile_picked_hmixfoldedf_none_p_kernel(
 
         z_pairs = keep.tile([P, 2, S, 2], BF16, name="z_pairs")
         ds_rows = []
+        gates = keep.tile([P, PACK, W], F32, name="gates", tag="gates_then_w3", align_bytes=64)
+        pas = keep.tile([P, PACK, W], F32, name="pas")
 
         def apply_gain(t):
             nc.vector.tensor_scalar(
@@ -145,26 +158,25 @@ def tile_picked_hmixfoldedf_none_p_kernel(
             ds_rows.append(ds)
             if t == 0:
                 nc.vector.tensor_copy(ds[:], y_banks[t][:])
+                two_codes = pick_words("two_codes", two_l)
                 deal(nc.vector.tensor_copy, w2_grouped[:], w2_raw, 0, 4)
                 quantize(w2_codes[:], w2_scales[:], w2_grouped[:].rearrange("p t m j -> p (t m j)"))
             else:
                 nc.scalar.copy(ds[:], y_banks[t][:])
-            gate = keep.tile([P, W], F32, name=f"gate{t}")
-            pa = keep.tile([P, W], F32, name=f"pa{t}")
-            nc.scalar.activation(gate[:], ds[:].indirect(n2_l[:]), ACT.Sigmoid)
-            nc.scalar.activation(pa[:], ds[:].indirect(n1_l[:]), ACT.Copy)
-            if t == 2:
-                ra = keep.tile([P, W], F32, name="ra")
-                nc.vector.tensor_tensor(ra[:], pa[:], gate[:], ALU.mult)
-            else:
-                nc.vector.tensor_tensor(ds[:].indirect(n2_l[:]), pa[:], gate[:], ALU.mult)
-            if t == 3:
-                nc.scalar.activation(ds_rows[2][:].indirect(n2_l[:]), ra[:], ACT.Copy)
-                apply_gain(2)
-            if t != 2:
+            gate, pa = gates[:, t, :], pas[:, t, :]
+            nc.scalar.activation(gate, ds[:].indirect(n2_l[:]), ACT.Sigmoid)
+            nc.scalar.activation(pa, ds[:].indirect(n1_l[:]), ACT.Copy)
+            if t < 2:
+                nc.vector.tensor_tensor(ds[:].indirect(n2_l[:]), pa, gate, ALU.mult)
                 apply_gain(t)
+        ra = keep.tile([P, 2, W], F32, name="ra")
+        nc.vector.tensor_tensor(ra[:], pas[:, 2:4, :], gates[:, 2:4, :], ALU.mult)
+        nc.scalar.activation(ds_rows[2][:].indirect(n2_l[:]), ra[:, 0, :], ACT.Copy)
+        nc.vector.tensor_copy(ds_rows[3][:].indirect(n2_l[:]), ra[:, 1, :])
+        apply_gain(3)
+        apply_gain(2)
 
-        w3_low = keep.tile([P, 2, P, PACK], BF16, name="w3_low", align_bytes=64)
+        w3_low = keep.tile([P, 2, P, PACK], BF16, name="w3_low", tag="gates_then_w3", align_bytes=64)
         deal(nc.scalar.copy, w3_low[:], w3_raw, 0, 2)
         quantize(w3_codes[:, :HALF], w3_scales[:, :HALF], w3_low[:].rearrange("p t m j -> p (t m j)"))
 
@@ -186,7 +198,7 @@ def tile_picked_hmixfoldedf_none_p_kernel(
                 lhsT=w3_codes[:, cols].bitcast(FP8X4),
                 lhsT_scale=w3_scales[:, cols],
                 rhs=two_codes[:].bitcast(FP8X4),
-                rhs_scale=x_planes[:, S:],
+                rhs_scale=two_scales[:],
                 start=True,
                 stop=False,
             )

@@ -43,18 +43,17 @@ def tile_picked_hmixfoldedf_none_p_kernel(
             nc.gpsimd.dma_start(dst[:], src.rearrange("(p t) o -> p (t o)", t=PACK))
             return dst
 
-        x_bytes = keep.tile([P, T], U8, name="x_bytes", tag="bytes_then_w2")
-        nc.vector.memset(x_bytes[:].bitcast(I32), 0)
-        nc.scalar.dma_start(x_bytes[0:P:8, :].bitcast(I32), x_scales[0].bitcast(I32))
-
         offs_l = load_list("offs_l", offs)
         two_l = load_list("two_l", two)
+        n2_l = load_list("n2_l", n2)
+        n1_l = load_list("n1_l", n1)
+        x_bytes = keep.tile([P, T], U8, name="x_bytes", tag="bytes_then_w2")
+        nc.vector.memset(x_bytes[:].bitcast(I32), 0)
+        nc.sync.dma_start(x_bytes[0:P:8, :].bitcast(I32), x_scales[0].bitcast(I32))
         x_codes = keep.tile([P, T], U32, name="x_codes")
         nc.sync.dma_start(
             x_codes[:].bitcast(I32), x_words[0].rearrange("p n r -> p (n r)").bitcast(I32)
         )
-        n2_l = load_list("n2_l", n2)
-        n1_l = load_list("n1_l", n1)
         w1_raw = [
             load_weight(f"w1_raw{c}", w1[:, c * HALF : (c + 1) * HALF], f"w1_raw{c}") for c in range(2)
         ]
@@ -62,8 +61,8 @@ def tile_picked_hmixfoldedf_none_p_kernel(
         rate = load_rows("rate", tau)
         rate2 = load_rows("rate2", tau2)
 
-        h_rows = [keep.tile([P, 2 * S], F32, name=f"h_rows{t}") for t in range(PACK)]
-        for t in range(PACK):
+        h_rows = [keep.tile([P, 2 * S if t < PACK - 1 else S], F32, name=f"h_rows{t}") for t in range(PACK)]
+        for t in range(PACK - 1):
             nc.vector.memset(h_rows[t][:, S:], 0.0)
 
         warm = keep.tile([P, 1], F32, name="warm")
@@ -86,14 +85,15 @@ def tile_picked_hmixfoldedf_none_p_kernel(
                 queue.dma_start(plane[r:P:32, :].bitcast(I32), picked[8 * r : P : 32, :].bitcast(I32))
             return plane
 
-        def pick_words(name, offsets):
-            codes = keep.tile([P, S], U32, name=name, align_bytes=64)
-            nc.vector.tensor_copy(codes[:], x_codes[:].indirect(offsets[:]))
+        def pick_words(name, offsets, tag):
+            codes = keep.tile([P, 16 * offsets.shape[1]], U32, name=name, tag=tag, align_bytes=64)
+            nc.vector.tensor_copy(codes[:], x_codes[:].indirect(offsets))
             return codes
 
         xq_scales = place_bytes("xq_scales", pick_bytes("xq_picked", offs_l, "bytes_then_w3"), nc.scalar)
         two_picked = pick_bytes("two_picked", two_l, "two_picked")
-        xq_codes = pick_words("xq_codes", offs_l)
+        xq_codes = pick_words("xq_codes", offs_l[:], "xq_codes")
+        two_codes = [pick_words("two_codes0", two_l[:, :16], "two_codes0")]
         w2_raw = load_weight("w2_raw", w2, "bytes_then_w2")
         w3_raw = load_weight("w3_raw", w3, "bytes_then_w3")
         two_scales = place_bytes("two_scales", two_picked, nc.sync)
@@ -110,10 +110,10 @@ def tile_picked_hmixfoldedf_none_p_kernel(
             nc.vector.quantize_mx(out=codes.bitcast(FP8X4), scales=scales, in_=grouped)
 
         w1_grouped = [
-            keep.tile([P, PACK, 64, PACK], BF16, name=f"w1_grouped{c}", align_bytes=64) for c in range(2)
+            keep.tile([P, PACK, 64, PACK], BF16, name=f"w1_grouped{c}", tag=f"w1_grouped{c}", align_bytes=64) for c in range(2)
         ]
         deal(nc.scalar.copy, w1_grouped[0][:], w1_raw[0], 0, 4)
-        deal(nc.scalar.copy, w1_grouped[1][:, 0:2], w1_raw[1], 0, 2)
+        deal(nc.vector.tensor_copy, w1_grouped[1][:, 0:2], w1_raw[1], 0, 2)
         deal(nc.scalar.copy, w1_grouped[1][:, 2:4], w1_raw[1], 2, 4)
         w1_codes = keep.tile([P, H], U32, name="w1_codes", align_bytes=64)
         w1_scales = keep.tile([P, H], U8, name="w1_scales", align_bytes=64)
@@ -137,82 +137,87 @@ def tile_picked_hmixfoldedf_none_p_kernel(
             )
             y_banks.append(bank)
 
+        two_codes.append(pick_words("two_codes1", two_l[:, 16:], "w1_grouped1"))
+
         w2_grouped = keep.tile([P, PACK, P, PACK], BF16, name="w2_grouped", align_bytes=64)
         w2_codes = keep.tile([P, N], U32, name="w2_codes", align_bytes=64)
         w2_scales = keep.tile([P, N], U8, name="w2_scales", align_bytes=64)
         w3_codes = keep.tile([P, N], U32, name="w3_codes", align_bytes=64)
         w3_scales = keep.tile([P, N], U8, name="w3_scales", align_bytes=64)
 
-        z_pairs = keep.tile([P, 2, S, 2], BF16, name="z_pairs")
-        ds_rows = []
-        gates = keep.tile([P, PACK, W], F32, name="gates", tag="gates_then_w3", align_bytes=64)
-        pas = keep.tile([P, PACK, W], F32, name="pas")
+        ds_rows = [keep.tile([P, S], F32, name=f"ds{t}") for t in range(PACK)]
+        last = PACK - 1
+        for t in range(PACK):
+            ds = ds_rows[t]
+            if t > 0:
+                nc.scalar.copy(ds[:], y_banks[t][:])
+            else:
+                nc.vector.tensor_copy(ds[:], y_banks[t][:])
+                deal(nc.vector.tensor_copy, w2_grouped[:], w2_raw, 0, 4)
+                quantize(w2_codes[:], w2_scales[:], w2_grouped[:].rearrange("p t m j -> p (t m j)"))
+            gate = keep.tile([P, W], F32, name=f"gate{t}", tag=f"gate{t}")
+            pa = keep.tile([P, W], F32, name=f"pa{t}", tag=f"pa{t}", align_bytes=64)
+            nc.scalar.activation(gate[:], ds[:].indirect(n2_l[:]), ACT.Sigmoid)
+            nc.scalar.activation(pa[:], ds[:].indirect(n1_l[:]), ACT.Copy)
+            if t < last:
+                nc.vector.tensor_tensor(ds[:].indirect(n2_l[:]), pa[:], gate[:], ALU.mult)
+            else:
+                ra = keep.tile([P, W], F32, name="ra")
+                nc.vector.tensor_tensor(ra[:], pa[:], gate[:], ALU.mult)
+                nc.scalar.activation(ds[:].indirect(n2_l[:]), ra[:], ACT.Copy)
 
-        def apply_gain(t):
+        w3_low = keep.tile([P, 2, P, PACK], BF16, name="w3_low", tag=f"pa{last}", align_bytes=64)
+        deal(nc.vector.tensor_copy, w3_low[:], w3_raw, 0, 2)
+        quantize(w3_codes[:, :HALF], w3_scales[:, :HALF], w3_low[:].rearrange("p t m j -> p (t m j)"))
+        z_pairs = keep.tile([P, 2, S, 2], BF16, name="z_pairs", tag=f"gate{last}")
+        for t in range(PACK):
             nc.vector.tensor_scalar(
                 z_pairs[:, t // 2, :, t % 2], ds_rows[t][:], gain[:, t : t + 1], None, ALU.mult
             )
 
-        for t in range(PACK):
-            ds = keep.tile([P, S], F32, name=f"ds{t}")
-            ds_rows.append(ds)
-            if t == 0:
-                nc.vector.tensor_copy(ds[:], y_banks[t][:])
-                two_codes = pick_words("two_codes", two_l)
-                deal(nc.vector.tensor_copy, w2_grouped[:], w2_raw, 0, 4)
-                quantize(w2_codes[:], w2_scales[:], w2_grouped[:].rearrange("p t m j -> p (t m j)"))
-            else:
-                nc.scalar.copy(ds[:], y_banks[t][:])
-            gate, pa = gates[:, t, :], pas[:, t, :]
-            nc.scalar.activation(gate, ds[:].indirect(n2_l[:]), ACT.Sigmoid)
-            nc.scalar.activation(pa, ds[:].indirect(n1_l[:]), ACT.Copy)
-            if t < 2:
-                nc.vector.tensor_tensor(ds[:].indirect(n2_l[:]), pa, gate, ALU.mult)
-                apply_gain(t)
-        ra = keep.tile([P, 2, W], F32, name="ra")
-        nc.vector.tensor_tensor(ra[:], pas[:, 2:4, :], gates[:, 2:4, :], ALU.mult)
-        nc.scalar.activation(ds_rows[2][:].indirect(n2_l[:]), ra[:, 0, :], ACT.Copy)
-        nc.vector.tensor_copy(ds_rows[3][:].indirect(n2_l[:]), ra[:, 1, :])
-        apply_gain(3)
-        apply_gain(2)
-
-        w3_low = keep.tile([P, 2, P, PACK], BF16, name="w3_low", tag="gates_then_w3", align_bytes=64)
-        deal(nc.scalar.copy, w3_low[:], w3_raw, 0, 2)
-        quantize(w3_codes[:, :HALF], w3_scales[:, :HALF], w3_low[:].rearrange("p t m j -> p (t m j)"))
-
-        z_grouped = keep.tile([P, S * PACK], BF16, name="z_grouped", tag="late", align_bytes=64)
-        nc.vector.tensor_copy(
-            z_grouped[:].bitcast(I32).rearrange("p (c u) -> p c u", u=2),
-            z_pairs[:].rearrange("p u c e -> p u (c e)").bitcast(I32).rearrange("p u c -> p c u"),
-        )
         z_codes = keep.tile([P, S], U32, name="z_codes", align_bytes=64)
         z_scales = keep.tile([P, S], U8, name="z_scales", align_bytes=64)
-        quantize(z_codes[:], z_scales[:], z_grouped[:])
+        pair_words = z_pairs[:].rearrange("p u c e -> p u (c e)").bitcast(U32).rearrange("p u c -> p c u")
+        halves = [slice(i * HALF, (i + 1) * HALF) for i in range(2)]
+        z_grouped = [
+            keep.tile([P, HALF * PACK], BF16, name=f"z_grouped{i}", tag=f"z_grouped{i}", align_bytes=64)
+            for i in range(2)
+        ]
+        nc.vector.tensor_copy(
+            z_grouped[0][:].bitcast(I32).rearrange("p (c u) -> p c u", u=2),
+            z_pairs[:].rearrange("p u c e -> p u (c e)").bitcast(I32).rearrange("p u c -> p c u")[:, halves[0], :],
+        )
+        nc.scalar.copy(
+            z_grouped[1][:].bitcast(U32).rearrange("p (c u) -> p c u", u=2), pair_words[:, halves[1], :]
+        )
+        for i in range(2):
+            quantize(z_codes[:, halves[i]], z_scales[:, halves[i]], z_grouped[i][:])
 
         h_banks = [psum.tile([P, S], F32, name=f"h_bank{t}") for t in range(PACK)]
 
         def plain_pass(t):
             cols = slice(t * P, (t + 1) * P)
-            nc.tensor.matmul_mx(
-                out=h_banks[t][:],
-                lhsT=w3_codes[:, cols].bitcast(FP8X4),
-                lhsT_scale=w3_scales[:, cols],
-                rhs=two_codes[:].bitcast(FP8X4),
-                rhs_scale=two_scales[:],
-                start=True,
-                stop=False,
-            )
+            for i in range(2):
+                nc.tensor.matmul_mx(
+                    out=h_banks[t][:, halves[i]],
+                    lhsT=w3_codes[:, cols].bitcast(FP8X4),
+                    lhsT_scale=w3_scales[:, cols],
+                    rhs=two_codes[i][:].bitcast(FP8X4),
+                    rhs_scale=two_scales[:, halves[i]],
+                    start=i == 0,
+                    stop=False,
+                )
 
-        def hidden_pass(t):
+        def hidden_pass(t, places=slice(0, S)):
             cols = slice(t * P, (t + 1) * P)
             nc.tensor.matmul_mx(
-                out=h_banks[t][:],
+                out=h_banks[t][:, places],
                 lhsT=w2_codes[:, cols].bitcast(FP8X4),
                 lhsT_scale=w2_scales[:, cols],
-                rhs=z_codes[:].bitcast(FP8X4),
-                rhs_scale=z_scales[:],
+                rhs=z_codes[:, places].bitcast(FP8X4),
+                rhs_scale=z_scales[:, places],
                 start=False,
-                stop=True,
+                stop=places.stop == S,
             )
 
         biases = []
@@ -223,16 +228,20 @@ def tile_picked_hmixfoldedf_none_p_kernel(
             nc.vector.tensor_scalar(
                 h_rows[t][:, :S], h_banks[t][:], 1.0, None, ALU.mult, ALU.max, accum_out=top
             )
-            nc.vector.tensor_scalar(bias, top, neg_rate[:, t : t + 1], None, ALU.mult)
+            if t == 0:
+                nc.scalar.activation(bias, top, ACT.Copy, scale=neg_rate[:, t : t + 1])
+            else:
+                nc.vector.tensor_scalar(bias, top, neg_rate[:, t : t + 1], None, ALU.mult)
             nc.vector.tensor_reduce(low, h_banks[t][:], mybir.AxisListType.X, ALU.min)
             nc.vector.tensor_scalar(bias2, low, rate2[:, t : t + 1], None, ALU.mult)
             biases.append((bias, bias2))
 
         plain_pass(0)
         plain_pass(1)
-        hidden_pass(0)
+        hidden_pass(0, halves[0])
+        hidden_pass(0, halves[1])
         hidden_pass(1)
-        w3_high = keep.tile([P, 2, P, PACK], BF16, name="w3_high", tag="late", align_bytes=64)
+        w3_high = keep.tile([P, 2, P, PACK], BF16, name="w3_high", tag="z_grouped1", align_bytes=64)
         deal(nc.vector.tensor_copy, w3_high[:], w3_raw, 2, 4)
         row_stats(0)
         quantize(w3_codes[:, HALF:], w3_scales[:, HALF:], w3_high[:].rearrange("p t m j -> p (t m j)"))
@@ -243,29 +252,29 @@ def tile_picked_hmixfoldedf_none_p_kernel(
             row_stats(t)
 
         out_rows = out.rearrange("(p t) n -> t p n", t=PACK)
+        def fetch_exp(name, t, places, offsets, bias, scale):
+            values = keep.tile([P, places.stop - places.start], F32, name=name)
+            nc.scalar.activation(
+                values[:],
+                h_rows[t][:].indirect(offsets[:, places.start // 16 : places.stop // 16]),
+                ACT.Exp,
+                bias=bias,
+                scale=scale[:, t : t + 1],
+            )
+            return values
+
         for t in range(PACK):
             bias, bias2 = biases[t]
-            ea = keep.tile([P, S], F32, name=f"ea{t}")
-            nc.scalar.activation(
-                ea[:], h_rows[t][:].indirect(n3_l[:]), ACT.Exp, bias=bias, scale=rate[:, t : t + 1]
-            )
-            pieces = 2 if t == PACK - 1 else 1
-            width = S // pieces
-            for i in range(pieces):
-                cols = slice(i * width, (i + 1) * width)
-                ea2 = keep.tile([P, width], F32, name=f"ea2_{t}_{i}")
-                nc.scalar.activation(
-                    ea2[:],
-                    h_rows[t][:].indirect(n4_l[:, i * width // 16 : (i + 1) * width // 16]),
-                    ACT.Exp,
-                    bias=bias2,
-                    scale=neg_rate2[:, t : t + 1],
-                )
+            pieces = [slice(0, S)] if t < last else [slice(0, 256), slice(256, 384), slice(384, 512)]
+            adder = nc.vector if t == PACK - 1 else nc.gpsimd
+            for i, places in enumerate(pieces):
+                width = places.stop - places.start
+                ea = fetch_exp(f"ea_{t}_{i}", t, places, n3_l, bias, rate)
+                ea2 = fetch_exp(f"ea2_{t}_{i}", t, places, n4_l, bias2, neg_rate2)
                 both = keep.tile([P, width], F32, name=f"both_{t}_{i}")
-                adder = nc.vector if t == PACK - 1 else nc.gpsimd
-                adder.tensor_tensor(both[:], ea[:, cols], ea2[:], ALU.add)
+                adder.tensor_tensor(both[:], ea[:], ea2[:], ALU.add)
                 result = keep.tile([P, width], F32, name=f"result_{t}_{i}")
                 nc.vector.scalar_tensor_tensor(
-                    result[:], h_banks[t][:, cols], 1.5, both[:], ALU.mult, ALU.mult
+                    result[:], h_banks[t][:, places], 1.5, both[:], ALU.mult, ALU.mult
                 )
-                nc.sync.dma_start(out_rows[t][:, cols], result[:])
+                nc.sync.dma_start(out_rows[t][:, places], result[:])

@@ -17,7 +17,15 @@ ACT = mybir.ActivationFunctionType
 
 P = 128
 PACK = 4
+LAST = PACK - 1
+GROUP = 16
+QUADRANT = 32
+BLOCK_PARTITIONS = 8
 HALF = 256
+HALVES = [slice(0, HALF), slice(HALF, 2 * HALF)]
+ALL_PLACES = slice(0, S)
+SCALAR_SCATTERS = 2
+TAIL_PIECES = [slice(0, 256), slice(256, 384), slice(384, 512)]
 
 
 def tile_picked_hmixfoldedf_none_p_kernel(
@@ -49,24 +57,22 @@ def tile_picked_hmixfoldedf_none_p_kernel(
         n1_l = load_list("n1_l", n1)
         x_bytes = keep.tile([P, T], U8, name="x_bytes", tag="bytes_then_w2")
         nc.vector.memset(x_bytes[:].bitcast(I32), 0)
-        nc.sync.dma_start(x_bytes[0:P:8, :].bitcast(I32), x_scales[0].bitcast(I32))
+        nc.sync.dma_start(x_bytes[0:P:BLOCK_PARTITIONS, :].bitcast(I32), x_scales[0].bitcast(I32))
         x_codes = keep.tile([P, T], U32, name="x_codes")
-        nc.sync.dma_start(
-            x_codes[:].bitcast(I32), x_words[0].rearrange("p n r -> p (n r)").bitcast(I32)
-        )
-        w1_raw = [
-            load_weight(f"w1_raw{c}", w1[:, c * HALF : (c + 1) * HALF], f"w1_raw{c}") for c in range(2)
-        ]
+        nc.sync.dma_start(x_codes[:].bitcast(I32), x_words[0].rearrange("p n r -> p (n r)").bitcast(I32))
+        w1_raw = [load_weight(f"w1_raw{c}", w1[:, HALVES[c]], f"w1_raw{c}") for c in range(2)]
         gain = load_rows("gain", gn)
         rate = load_rows("rate", tau)
         rate2 = load_rows("rate2", tau2)
 
-        h_rows = [keep.tile([P, 2 * S if t < PACK - 1 else S], F32, name=f"h_rows{t}") for t in range(PACK)]
-        for t in range(PACK - 1):
+        h_rows = [keep.tile([P, 2 * S if t < LAST else S], F32, name=f"h_rows{t}") for t in range(PACK)]
+        for t in range(LAST):
             nc.vector.memset(h_rows[t][:, S:], 0.0)
 
-        warm = keep.tile([P, 1], F32, name="warm")
-        nc.scalar.activation(warm[:], h_rows[0][:, S : S + 1], ACT.Sigmoid)
+        warm_in = keep.tile([P, 1], F32, name="warm_in")
+        warm_out = keep.tile([P, 1], F32, name="warm_out")
+        nc.vector.memset(warm_in[:], 0.0)
+        nc.scalar.activation(warm_out[:], warm_in[:], ACT.Sigmoid)
 
         neg_rate = keep.tile([P, PACK], F32, name="neg_rate")
         neg_rate2 = keep.tile([P, PACK], F32, name="neg_rate2")
@@ -79,21 +85,24 @@ def tile_picked_hmixfoldedf_none_p_kernel(
             return picked
 
         def place_bytes(name, picked, queue):
-            plane = keep.tile([P, S], U8, name=name, align_bytes=64)
-            nc.vector.memset(plane[:].bitcast(I32), 0)
-            for r in range(4):
-                queue.dma_start(plane[r:P:32, :].bitcast(I32), picked[8 * r : P : 32, :].bitcast(I32))
-            return plane
+            placed = keep.tile([P, S], U8, name=name, align_bytes=64)
+            nc.vector.memset(placed[:].bitcast(I32), 0)
+            for r in range(QUADRANT // BLOCK_PARTITIONS):
+                queue.dma_start(
+                    placed[r:P:QUADRANT, :].bitcast(I32),
+                    picked[BLOCK_PARTITIONS * r : P : QUADRANT, :].bitcast(I32),
+                )
+            return placed
 
         def pick_words(name, offsets, tag):
-            codes = keep.tile([P, 16 * offsets.shape[1]], U32, name=name, tag=tag, align_bytes=64)
+            codes = keep.tile([P, GROUP * offsets.shape[1]], U32, name=name, tag=tag, align_bytes=64)
             nc.vector.tensor_copy(codes[:], x_codes[:].indirect(offsets))
             return codes
 
         xq_scales = place_bytes("xq_scales", pick_bytes("xq_picked", offs_l, "bytes_then_w3"), nc.scalar)
         two_picked = pick_bytes("two_picked", two_l, "two_picked")
         xq_codes = pick_words("xq_codes", offs_l[:], "xq_codes")
-        two_codes = [pick_words("two_codes0", two_l[:, :16], "two_codes0")]
+        two_codes = [pick_words("two_codes0", two_l[:, : HALF // GROUP], "two_codes0")]
         w2_raw = load_weight("w2_raw", w2, "bytes_then_w2")
         w3_raw = load_weight("w3_raw", w3, "bytes_then_w3")
         two_scales = place_bytes("two_scales", two_picked, nc.sync)
@@ -109,8 +118,10 @@ def tile_picked_hmixfoldedf_none_p_kernel(
         def quantize(codes, scales, grouped):
             nc.vector.quantize_mx(out=codes.bitcast(FP8X4), scales=scales, in_=grouped)
 
+        half_m = HALF // PACK
         w1_grouped = [
-            keep.tile([P, PACK, 64, PACK], BF16, name=f"w1_grouped{c}", tag=f"w1_grouped{c}", align_bytes=64) for c in range(2)
+            keep.tile([P, PACK, half_m, PACK], BF16, name=f"w1_grouped{c}", tag=f"w1_grouped{c}", align_bytes=64)
+            for c in range(2)
         ]
         deal(nc.scalar.copy, w1_grouped[0][:], w1_raw[0], 0, 4)
         deal(nc.vector.tensor_copy, w1_grouped[1][:, 0:2], w1_raw[1], 0, 2)
@@ -120,10 +131,8 @@ def tile_picked_hmixfoldedf_none_p_kernel(
         y_banks = []
         for t in range(PACK):
             for c in range(2):
-                cols = slice(t * P + c * 64, t * P + (c + 1) * 64)
-                quantize(
-                    w1_codes[:, cols], w1_scales[:, cols], w1_grouped[c][:, t].rearrange("p m j -> p (m j)")
-                )
+                part = slice(t * P + c * half_m, t * P + (c + 1) * half_m)
+                quantize(w1_codes[:, part], w1_scales[:, part], w1_grouped[c][:, t].rearrange("p m j -> p (m j)"))
             cols = slice(t * P, (t + 1) * P)
             bank = psum.tile([P, S], F32, name=f"y_bank{t}")
             nc.tensor.matmul_mx(
@@ -137,7 +146,7 @@ def tile_picked_hmixfoldedf_none_p_kernel(
             )
             y_banks.append(bank)
 
-        two_codes.append(pick_words("two_codes1", two_l[:, 16:], "w1_grouped1"))
+        two_codes.append(pick_words("two_codes1", two_l[:, HALF // GROUP :], "w1_grouped1"))
 
         w2_grouped = keep.tile([P, PACK, P, PACK], BF16, name="w2_grouped", align_bytes=64)
         w2_codes = keep.tile([P, N], U32, name="w2_codes", align_bytes=64)
@@ -146,52 +155,48 @@ def tile_picked_hmixfoldedf_none_p_kernel(
         w3_scales = keep.tile([P, N], U8, name="w3_scales", align_bytes=64)
 
         ds_rows = [keep.tile([P, S], F32, name=f"ds{t}") for t in range(PACK)]
-        last = PACK - 1
-        for t in range(PACK):
-            ds = ds_rows[t]
-            if t > 0:
-                nc.scalar.copy(ds[:], y_banks[t][:])
-            else:
-                nc.vector.tensor_copy(ds[:], y_banks[t][:])
-                deal(nc.vector.tensor_copy, w2_grouped[:], w2_raw, 0, 4)
-                quantize(w2_codes[:], w2_scales[:], w2_grouped[:].rearrange("p t m j -> p (t m j)"))
-            gate = keep.tile([P, W], F32, name=f"gate{t}", tag=f"gate{t}")
-            pa = keep.tile([P, W], F32, name=f"pa{t}", tag=f"pa{t}", align_bytes=64)
-            nc.scalar.activation(gate[:], ds[:].indirect(n2_l[:]), ACT.Sigmoid)
-            nc.scalar.activation(pa[:], ds[:].indirect(n1_l[:]), ACT.Copy)
-            if t < last:
-                nc.vector.tensor_tensor(ds[:].indirect(n2_l[:]), pa[:], gate[:], ALU.mult)
-            else:
-                ra = keep.tile([P, W], F32, name="ra")
-                nc.vector.tensor_tensor(ra[:], pa[:], gate[:], ALU.mult)
-                nc.scalar.activation(ds[:].indirect(n2_l[:]), ra[:], ACT.Copy)
+        z_pairs = keep.tile([P, 2, S, 2], BF16, name="z_pairs")
 
-        w3_low = keep.tile([P, 2, P, PACK], BF16, name="w3_low", tag=f"pa{last}", align_bytes=64)
-        deal(nc.vector.tensor_copy, w3_low[:], w3_raw, 0, 2)
-        quantize(w3_codes[:, :HALF], w3_scales[:, :HALF], w3_low[:].rearrange("p t m j -> p (t m j)"))
-        z_pairs = keep.tile([P, 2, S, 2], BF16, name="z_pairs", tag=f"gate{last}")
-        for t in range(PACK):
+        def apply_gain(t):
             nc.vector.tensor_scalar(
                 z_pairs[:, t // 2, :, t % 2], ds_rows[t][:], gain[:, t : t + 1], None, ALU.mult
             )
 
+        for t in range(PACK):
+            ds = ds_rows[t]
+            nc.scalar.copy(ds[:], y_banks[t][:])
+            if t == 0:
+                deal(nc.vector.tensor_copy, w2_grouped[:], w2_raw, 0, 4)
+                quantize(w2_codes[:], w2_scales[:], w2_grouped[:].rearrange("p t m j -> p (t m j)"))
+            gate = keep.tile([P, W], F32, name=f"gate{t}")
+            pa = keep.tile([P, W], F32, name=f"pa{t}", tag=f"pa{t}", align_bytes=64)
+            nc.scalar.activation(gate[:], ds[:].indirect(n2_l[:]), ACT.Sigmoid)
+            nc.scalar.activation(pa[:], ds[:].indirect(n1_l[:]), ACT.Copy)
+            if t != SCALAR_SCATTERS:
+                nc.vector.tensor_tensor(ds[:].indirect(n2_l[:]), pa[:], gate[:], ALU.mult)
+            else:
+                ra = keep.tile([P, W], F32, name="ra")
+                nc.vector.tensor_tensor(ra[:], pa[:], gate[:], ALU.mult)
+                w3_low = keep.tile([P, 2, P, PACK], BF16, name="w3_low", tag=f"pa{t}", align_bytes=64)
+                deal(nc.vector.tensor_copy, w3_low[:], w3_raw, 0, 2)
+                quantize(w3_codes[:, :HALF], w3_scales[:, :HALF], w3_low[:].rearrange("p t m j -> p (t m j)"))
+            if t < SCALAR_SCATTERS:
+                apply_gain(t)
+        nc.scalar.activation(ds_rows[SCALAR_SCATTERS][:].indirect(n2_l[:]), ra[:], ACT.Copy)
+        apply_gain(LAST)
+        apply_gain(SCALAR_SCATTERS)
+
         z_codes = keep.tile([P, S], U32, name="z_codes", align_bytes=64)
         z_scales = keep.tile([P, S], U8, name="z_scales", align_bytes=64)
-        pair_words = z_pairs[:].rearrange("p u c e -> p u (c e)").bitcast(U32).rearrange("p u c -> p c u")
-        halves = [slice(i * HALF, (i + 1) * HALF) for i in range(2)]
         z_grouped = [
             keep.tile([P, HALF * PACK], BF16, name=f"z_grouped{i}", tag=f"z_grouped{i}", align_bytes=64)
             for i in range(2)
         ]
-        nc.vector.tensor_copy(
-            z_grouped[0][:].bitcast(I32).rearrange("p (c u) -> p c u", u=2),
-            z_pairs[:].rearrange("p u c e -> p u (c e)").bitcast(I32).rearrange("p u c -> p c u")[:, halves[0], :],
-        )
-        nc.scalar.copy(
-            z_grouped[1][:].bitcast(U32).rearrange("p (c u) -> p c u", u=2), pair_words[:, halves[1], :]
-        )
+        for i, (copy, word) in enumerate([(nc.vector.tensor_copy, I32), (nc.scalar.copy, U32)]):
+            pair_words = z_pairs[:].rearrange("p u c e -> p u (c e)").bitcast(word).rearrange("p u c -> p c u")
+            copy(z_grouped[i][:].bitcast(word).rearrange("p (c u) -> p c u", u=2), pair_words[:, HALVES[i], :])
         for i in range(2):
-            quantize(z_codes[:, halves[i]], z_scales[:, halves[i]], z_grouped[i][:])
+            quantize(z_codes[:, HALVES[i]], z_scales[:, HALVES[i]], z_grouped[i][:])
 
         h_banks = [psum.tile([P, S], F32, name=f"h_bank{t}") for t in range(PACK)]
 
@@ -199,16 +204,16 @@ def tile_picked_hmixfoldedf_none_p_kernel(
             cols = slice(t * P, (t + 1) * P)
             for i in range(2):
                 nc.tensor.matmul_mx(
-                    out=h_banks[t][:, halves[i]],
+                    out=h_banks[t][:, HALVES[i]],
                     lhsT=w3_codes[:, cols].bitcast(FP8X4),
                     lhsT_scale=w3_scales[:, cols],
                     rhs=two_codes[i][:].bitcast(FP8X4),
-                    rhs_scale=two_scales[:, halves[i]],
+                    rhs_scale=two_scales[:, HALVES[i]],
                     start=i == 0,
                     stop=False,
                 )
 
-        def hidden_pass(t, places=slice(0, S)):
+        def hidden_pass(t, places):
             cols = slice(t * P, (t + 1) * P)
             nc.tensor.matmul_mx(
                 out=h_banks[t][:, places],
@@ -220,43 +225,44 @@ def tile_picked_hmixfoldedf_none_p_kernel(
                 stop=places.stop == S,
             )
 
-        biases = []
+        stats = [keep.tile([P, 4], F32, name=f"stats{t}") for t in range(PACK)]
 
-        def row_stats(t):
-            stats = keep.tile([P, 4], F32, name=f"stats{t}")
-            top, low, bias, bias2 = (stats[:, i : i + 1] for i in range(4))
+        def copy_with_top(t):
+            top, bias = stats[t][:, 0:1], stats[t][:, 1:2]
             nc.vector.tensor_scalar(
                 h_rows[t][:, :S], h_banks[t][:], 1.0, None, ALU.mult, ALU.max, accum_out=top
             )
-            if t == 0:
-                nc.scalar.activation(bias, top, ACT.Copy, scale=neg_rate[:, t : t + 1])
-            else:
-                nc.vector.tensor_scalar(bias, top, neg_rate[:, t : t + 1], None, ALU.mult)
+            nc.vector.tensor_scalar(bias, top, neg_rate[:, t : t + 1], None, ALU.mult)
+
+        def find_low(t):
+            low, bias2 = stats[t][:, 2:3], stats[t][:, 3:4]
             nc.vector.tensor_reduce(low, h_banks[t][:], mybir.AxisListType.X, ALU.min)
             nc.vector.tensor_scalar(bias2, low, rate2[:, t : t + 1], None, ALU.mult)
-            biases.append((bias, bias2))
 
         plain_pass(0)
         plain_pass(1)
-        hidden_pass(0, halves[0])
-        hidden_pass(0, halves[1])
-        hidden_pass(1)
+        hidden_pass(0, HALVES[0])
+        hidden_pass(0, HALVES[1])
+        hidden_pass(1, ALL_PLACES)
         w3_high = keep.tile([P, 2, P, PACK], BF16, name="w3_high", tag="z_grouped1", align_bytes=64)
         deal(nc.vector.tensor_copy, w3_high[:], w3_raw, 2, 4)
-        row_stats(0)
+        copy_with_top(0)
         quantize(w3_codes[:, HALF:], w3_scales[:, HALF:], w3_high[:].rearrange("p t m j -> p (t m j)"))
-        for t in (2, 3):
+        find_low(0)
+        for t in range(2, PACK):
             plain_pass(t)
-            hidden_pass(t)
-        for t in (1, 2, 3):
-            row_stats(t)
+            hidden_pass(t, ALL_PLACES)
+        for t in range(1, PACK):
+            copy_with_top(t)
+            find_low(t)
 
         out_rows = out.rearrange("(p t) n -> t p n", t=PACK)
+
         def fetch_exp(name, t, places, offsets, bias, scale):
             values = keep.tile([P, places.stop - places.start], F32, name=name)
             nc.scalar.activation(
                 values[:],
-                h_rows[t][:].indirect(offsets[:, places.start // 16 : places.stop // 16]),
+                h_rows[t][:].indirect(offsets[:, places.start // GROUP : places.stop // GROUP]),
                 ACT.Exp,
                 bias=bias,
                 scale=scale[:, t : t + 1],
@@ -264,10 +270,9 @@ def tile_picked_hmixfoldedf_none_p_kernel(
             return values
 
         for t in range(PACK):
-            bias, bias2 = biases[t]
-            pieces = [slice(0, S)] if t < last else [slice(0, 256), slice(256, 384), slice(384, 512)]
-            adder = nc.vector if t == PACK - 1 else nc.gpsimd
-            for i, places in enumerate(pieces):
+            bias, bias2 = stats[t][:, 1:2], stats[t][:, 3:4]
+            adder = nc.gpsimd if t < LAST else nc.vector
+            for i, places in enumerate([ALL_PLACES] if t < LAST else TAIL_PIECES):
                 width = places.stop - places.start
                 ea = fetch_exp(f"ea_{t}_{i}", t, places, n3_l, bias, rate)
                 ea2 = fetch_exp(f"ea2_{t}_{i}", t, places, n4_l, bias2, neg_rate2)

from contextlib import ExitStack

import concourse.mybir as mybir

K, T, S, N, H, W = 512, 2048, 512, 512, 512, 256
FLOPS = 2 * S * (K * H + H * N + K * N)

F32 = mybir.dt.float32
BF16 = mybir.dt.bfloat16
I32 = mybir.dt.int32
U32 = mybir.dt.uint32
U16 = mybir.dt.uint16
U8 = mybir.dt.uint8
FP8X4 = mybir.dt.float8_e4m3fn_x4
ALU = mybir.AluOpType
ACT = mybir.ActivationFunctionType

P = 128
PACK = 4
LAST = PACK - 1
GROUP = 16
QUADRANT = 32
BLOCK_PARTITIONS = 8
HALF = 256
HALVES = [slice(0, HALF), slice(HALF, 2 * HALF)]
ALL_PLACES = slice(0, S)
SCALAR_SCATTERS = 2
TAIL_PIECES = [slice(0, 256), slice(256, 384), slice(384, 512)]


def tile_picked_hmixfoldedf_none_p_kernel(
    tc, x_words, x_scales, w1, gn, w2, w3, tau, tau2, offs, n1, n2, two, n3, n4, out
):
    nc = tc.nc
    with ExitStack() as ctx:
        keep = ctx.enter_context(tc.tile_pool(name="keep", bufs=1))
        psum = ctx.enter_context(tc.psum_pool(name="psum", bufs=1))

        def load_list(name, src):
            dst = keep.tile(list(src.shape), U16, name=name)
            nc.sync.dma_start(dst[:], src)
            return dst

        def load_weight(name, src, tag):
            dst = keep.tile([P, PACK, src.shape[1]], F32, name=name, tag=tag)
            nc.sync.dma_start(dst[:], src.rearrange("(p j) c -> p j c", j=PACK))
            return dst

        def load_rows(name, src):
            dst = keep.tile([P, PACK], F32, name=name)
            nc.gpsimd.dma_start(dst[:], src.rearrange("(p t) o -> p (t o)", t=PACK))
            return dst

        offs_l = load_list("offs_l", offs)
        two_l = load_list("two_l", two)
        n2_l = load_list("n2_l", n2)
        n1_l = load_list("n1_l", n1)
        x_bytes = keep.tile([P, T], U8, name="x_bytes", tag="bytes_then_w2")
        nc.vector.memset(x_bytes[:].bitcast(I32), 0)
        nc.sync.dma_start(x_bytes[0:P:BLOCK_PARTITIONS, :].bitcast(I32), x_scales[0].bitcast(I32))
        x_codes = keep.tile([P, T], U32, name="x_codes")
        nc.sync.dma_start(x_codes[:].bitcast(I32), x_words[0].rearrange("p n r -> p (n r)").bitcast(I32))
        w1_raw = [load_weight(f"w1_raw{c}", w1[:, HALVES[c]], f"w1_raw{c}") for c in range(2)]
        gain = load_rows("gain", gn)
        rate = load_rows("rate", tau)
        rate2 = load_rows("rate2", tau2)

        h_rows = [keep.tile([P, 2 * S if t < LAST else S], F32, name=f"h_rows{t}") for t in range(PACK)]
        for t in range(LAST):
            nc.vector.memset(h_rows[t][:, S:], 0.0)

        warm_in = keep.tile([P, 1], F32, name="warm_in")
        warm_out = keep.tile([P, 1], F32, name="warm_out")
        nc.vector.memset(warm_in[:], 0.0)
        nc.scalar.activation(warm_out[:], warm_in[:], ACT.Sigmoid)

        neg_rate = keep.tile([P, PACK], F32, name="neg_rate")
        neg_rate2 = keep.tile([P, PACK], F32, name="neg_rate2")
        nc.gpsimd.tensor_scalar(neg_rate[:], rate[:], -1.0, 0.0, ALU.mult, ALU.add)
        nc.gpsimd.tensor_scalar(neg_rate2[:], rate2[:], -1.0, 0.0, ALU.mult, ALU.add)

        def pick_bytes(name, offsets, tag):
            picked = keep.tile([P, S], U8, name=name, tag=tag)
            nc.vector.tensor_copy(picked[:], x_bytes[:].indirect(offsets[:]))
            return picked

        def place_bytes(name, picked, queue):
            placed = keep.tile([P, S], U8, name=name, align_bytes=64)
            nc.vector.memset(placed[:].bitcast(I32), 0)
            for r in range(QUADRANT // BLOCK_PARTITIONS):
                queue.dma_start(
                    placed[r:P:QUADRANT, :].bitcast(I32),
                    picked[BLOCK_PARTITIONS * r : P : QUADRANT, :].bitcast(I32),
                )
            return placed

        def pick_words(name, offsets, tag):
            codes = keep.tile([P, GROUP * offsets.shape[1]], U32, name=name, tag=tag, align_bytes=64)
            nc.vector.tensor_copy(codes[:], x_codes[:].indirect(offsets))
            return codes

        xq_scales = place_bytes("xq_scales", pick_bytes("xq_picked", offs_l, "bytes_then_w3"), nc.scalar)
        two_picked = pick_bytes("two_picked", two_l, "two_picked")
        xq_codes = pick_words("xq_codes", offs_l[:], "xq_codes")
        two_codes = [pick_words("two_codes0", two_l[:, : HALF // GROUP], "two_codes0")]
        w2_raw = load_weight("w2_raw", w2, "bytes_then_w2")
        w3_raw = load_weight("w3_raw", w3, "bytes_then_w3")
        two_scales = place_bytes("two_scales", two_picked, nc.sync)
        n3_l = load_list("n3_l", n3)
        n4_l = load_list("n4_l", n4)

        def deal(copy, grouped, raw, t0, t1):
            copy(
                grouped.rearrange("p t m j -> p m j t"),
                raw[:].rearrange("p j (m t) -> p m j t", t=PACK)[:, :, :, t0:t1],
            )

        def quantize(codes, scales, grouped):
            nc.vector.quantize_mx(out=codes.bitcast(FP8X4), scales=scales, in_=grouped)

        half_m = HALF // PACK
        w1_grouped = [
            keep.tile([P, PACK, half_m, PACK], BF16, name=f"w1_grouped{c}", tag=f"w1_grouped{c}", align_bytes=64)
            for c in range(2)
        ]
        deal(nc.scalar.copy, w1_grouped[0][:], w1_raw[0], 0, 4)
        deal(nc.vector.tensor_copy, w1_grouped[1][:, 0:2], w1_raw[1], 0, 2)
        deal(nc.scalar.copy, w1_grouped[1][:, 2:4], w1_raw[1], 2, 4)
        w1_codes = keep.tile([P, H], U32, name="w1_codes", align_bytes=64)
        w1_scales = keep.tile([P, H], U8, name="w1_scales", align_bytes=64)
        y_banks = []
        for t in range(PACK):
            for c in range(2):
                part = slice(t * P + c * half_m, t * P + (c + 1) * half_m)
                quantize(w1_codes[:, part], w1_scales[:, part], w1_grouped[c][:, t].rearrange("p m j -> p (m j)"))
            cols = slice(t * P, (t + 1) * P)
            bank = psum.tile([P, S], F32, name=f"y_bank{t}")
            nc.tensor.matmul_mx(
                out=bank[:],
                lhsT=w1_codes[:, cols].bitcast(FP8X4),
                lhsT_scale=w1_scales[:, cols],
                rhs=xq_codes[:].bitcast(FP8X4),
                rhs_scale=xq_scales[:],
                start=True,
                stop=True,
            )
            y_banks.append(bank)

        two_codes.append(pick_words("two_codes1", two_l[:, HALF // GROUP :], "w1_grouped1"))

        w2_grouped = keep.tile([P, PACK, P, PACK], BF16, name="w2_grouped", align_bytes=64)
        w2_codes = keep.tile([P, N], U32, name="w2_codes", align_bytes=64)
        w2_scales = keep.tile([P, N], U8, name="w2_scales", align_bytes=64)
        w3_codes = keep.tile([P, N], U32, name="w3_codes", align_bytes=64)
        w3_scales = keep.tile([P, N], U8, name="w3_scales", align_bytes=64)

        ds_rows = [keep.tile([P, S], F32, name=f"ds{t}") for t in range(PACK)]
        z_pairs = keep.tile([P, 2, S, 2], BF16, name="z_pairs")

        def apply_gain(t):
            nc.vector.tensor_scalar(
                z_pairs[:, t // 2, :, t % 2], ds_rows[t][:], gain[:, t : t + 1], None, ALU.mult
            )

        for t in range(PACK):
            ds = ds_rows[t]
            nc.scalar.copy(ds[:], y_banks[t][:])
            if t == 0:
                deal(nc.vector.tensor_copy, w2_grouped[:], w2_raw, 0, 4)
                quantize(w2_codes[:], w2_scales[:], w2_grouped[:].rearrange("p t m j -> p (t m j)"))
            gate = keep.tile([P, W], F32, name=f"gate{t}")
            pa = keep.tile([P, W], F32, name=f"pa{t}", tag=f"pa{t}", align_bytes=64)
            nc.scalar.activation(gate[:], ds[:].indirect(n2_l[:]), ACT.Sigmoid)
            nc.scalar.activation(pa[:], ds[:].indirect(n1_l[:]), ACT.Copy)
            if t != SCALAR_SCATTERS:
                nc.vector.tensor_tensor(ds[:].indirect(n2_l[:]), pa[:], gate[:], ALU.mult)
            else:
                ra = keep.tile([P, W], F32, name="ra")
                nc.vector.tensor_tensor(ra[:], pa[:], gate[:], ALU.mult)
                w3_low = keep.tile([P, 2, P, PACK], BF16, name="w3_low", tag=f"pa{t}", align_bytes=64)
                deal(nc.vector.tensor_copy, w3_low[:], w3_raw, 0, 2)
                quantize(w3_codes[:, :HALF], w3_scales[:, :HALF], w3_low[:].rearrange("p t m j -> p (t m j)"))
            if t < SCALAR_SCATTERS:
                apply_gain(t)
        nc.scalar.activation(ds_rows[SCALAR_SCATTERS][:].indirect(n2_l[:]), ra[:], ACT.Copy)
        apply_gain(LAST)
        apply_gain(SCALAR_SCATTERS)

        z_codes = keep.tile([P, S], U32, name="z_codes", align_bytes=64)
        z_scales = keep.tile([P, S], U8, name="z_scales", align_bytes=64)
        z_grouped = [
            keep.tile([P, HALF * PACK], BF16, name=f"z_grouped{i}", tag=f"z_grouped{i}", align_bytes=64)
            for i in range(2)
        ]
        for i, (copy, word) in enumerate([(nc.vector.tensor_copy, I32), (nc.scalar.copy, U32)]):
            pair_words = z_pairs[:].rearrange("p u c e -> p u (c e)").bitcast(word).rearrange("p u c -> p c u")
            copy(z_grouped[i][:].bitcast(word).rearrange("p (c u) -> p c u", u=2), pair_words[:, HALVES[i], :])
        for i in range(2):
            quantize(z_codes[:, HALVES[i]], z_scales[:, HALVES[i]], z_grouped[i][:])

        h_banks = [psum.tile([P, S], F32, name=f"h_bank{t}") for t in range(PACK)]

        def plain_pass(t):
            cols = slice(t * P, (t + 1) * P)
            for i in range(2):
                nc.tensor.matmul_mx(
                    out=h_banks[t][:, HALVES[i]],
                    lhsT=w3_codes[:, cols].bitcast(FP8X4),
                    lhsT_scale=w3_scales[:, cols],
                    rhs=two_codes[i][:].bitcast(FP8X4),
                    rhs_scale=two_scales[:, HALVES[i]],
                    start=i == 0,
                    stop=False,
                )

        def hidden_pass(t, places):
            cols = slice(t * P, (t + 1) * P)
            nc.tensor.matmul_mx(
                out=h_banks[t][:, places],
                lhsT=w2_codes[:, cols].bitcast(FP8X4),
                lhsT_scale=w2_scales[:, cols],
                rhs=z_codes[:, places].bitcast(FP8X4),
                rhs_scale=z_scales[:, places],
                start=False,
                stop=places.stop == S,
            )

        stats = [keep.tile([P, 4], F32, name=f"stats{t}") for t in range(PACK)]

        def copy_with_top(t):
            top, bias = stats[t][:, 0:1], stats[t][:, 1:2]
            nc.vector.tensor_scalar(
                h_rows[t][:, :S], h_banks[t][:], 1.0, None, ALU.mult, ALU.max, accum_out=top
            )
            nc.vector.tensor_scalar(bias, top, neg_rate[:, t : t + 1], None, ALU.mult)

        def find_low(t):
            low, bias2 = stats[t][:, 2:3], stats[t][:, 3:4]
            nc.vector.tensor_reduce(low, h_banks[t][:], mybir.AxisListType.X, ALU.min)
            nc.vector.tensor_scalar(bias2, low, rate2[:, t : t + 1], None, ALU.mult)

        plain_pass(0)
        plain_pass(1)
        hidden_pass(0, HALVES[0])
        hidden_pass(0, HALVES[1])
        hidden_pass(1, ALL_PLACES)
        w3_high = keep.tile([P, 2, P, PACK], BF16, name="w3_high", tag="z_grouped1", align_bytes=64)
        deal(nc.vector.tensor_copy, w3_high[:], w3_raw, 2, 4)
        copy_with_top(0)
        quantize(w3_codes[:, HALF:], w3_scales[:, HALF:], w3_high[:].rearrange("p t m j -> p (t m j)"))
        find_low(0)
        for t in range(2, PACK):
            plain_pass(t)
            hidden_pass(t, ALL_PLACES)
        for t in range(1, PACK):
            copy_with_top(t)
            find_low(t)

        out_rows = out.rearrange("(p t) n -> t p n", t=PACK)

        def fetch_exp(name, t, places, offsets, bias, scale):
            values = keep.tile([P, places.stop - places.start], F32, name=name)
            nc.scalar.activation(
                values[:],
                h_rows[t][:].indirect(offsets[:, places.start // GROUP : places.stop // GROUP]),
                ACT.Exp,
                bias=bias,
                scale=scale[:, t : t + 1],
            )
            return values

        for t in range(PACK):
            bias, bias2 = stats[t][:, 1:2], stats[t][:, 3:4]
            adder = nc.gpsimd if t < LAST else nc.vector
            for i, places in enumerate([ALL_PLACES] if t < LAST else TAIL_PIECES):
                width = places.stop - places.start
                ea = fetch_exp(f"ea_{t}_{i}", t, places, n3_l, bias, rate)
                ea2 = fetch_exp(f"ea2_{t}_{i}", t, places, n4_l, bias2, neg_rate2)
                both = keep.tile([P, width], F32, name=f"both_{t}_{i}")
                adder.tensor_tensor(both[:], ea[:], ea2[:], ALU.add)
                result = keep.tile([P, width], F32, name=f"result_{t}_{i}")
                nc.vector.scalar_tensor_tensor(
                    result[:], h_banks[t][:, places], 1.5, both[:], ALU.mult, ALU.mult
                )
                nc.sync.dma_start(out_rows[t][:, places], result[:])
